import numpy as np
import ml_dtypes


def mxq(x, axis, fmt="e4m3"):
    dtype, down = {"e4m3": (ml_dtypes.float8_e4m3fn, 7), "e5m2": (ml_dtypes.float8_e5m2, 14)}[fmt]
    v = np.moveaxis(np.asarray(x, np.float32).astype(ml_dtypes.bfloat16).astype(np.float64), axis, -1)
    blocks = v.reshape(v.shape[:-1] + (-1, 32))
    amax = np.abs(blocks).max(-1, keepdims=True)
    byte = np.maximum(np.where(amax > 0, np.frexp(amax)[1] - 1 + 127, 0) - down, 1)
    scale = np.exp2(byte - 127.0)
    codes = (blocks / scale).astype(np.float32).astype(dtype).astype(np.float64)
    return np.moveaxis((codes * scale).reshape(v.shape), -1, axis)


WIDE = False


def mx_kscale(k):
    if not WIDE:
        return np.ones(k)
    levels = np.array([10, -10, 5, -5, 0])
    if k % 512:
        return np.exp2(np.random.permutation(np.resize(levels, k // 32))).repeat(32)
    a = np.empty((k // 512, 16))
    for p in range(k // 512):
        a[p, :8] = np.random.permutation(np.resize(levels, 8))
        for g in range(8):
            far = levels[np.abs(levels - a[p, g]) >= 10]
            a[p, g + 8] = far[np.random.randint(len(far))]
    return np.exp2(a.ravel()).repeat(32)


BF16 = ml_dtypes.bfloat16


def bf(x):
    return np.asarray(x, np.float32).astype(BF16)


def f64(x):
    return np.asarray(x).astype(np.float64)


E2M1 = np.array([0.0, 0.5, 1.0, 1.5, 2.0, 3.0, 4.0, 6.0, -0.0, -0.5, -1.0, -1.5, -2.0, -3.0, -4.0, -6.0])


def pack_weight(w, fmt):
    k, n = w.shape
    w = f64(bf(w)).reshape(k // 32, 32, n)
    amax = np.abs(w).max(1)
    if fmt == "e4m3":
        byte = np.frexp(amax)[1] - 1 + 127 - 7
    else:
        mant, ex = np.frexp(amax / 6.0)
        byte = np.where(mant > 0.5, ex, ex - 1) + 127
    byte = np.clip(np.where(amax > 0, byte, 1), 1, 254)
    scaled = (w * np.exp2(127.0 - byte)[:, None, :]).reshape(k, n).astype(np.float32)
    by_word = np.ascontiguousarray(scaled.reshape(k // 512, 128, 4, n).transpose(0, 1, 3, 2))
    if fmt == "e4m3":
        words = by_word.astype(ml_dtypes.float8_e4m3fn).view(np.uint8)
    else:
        c = by_word.astype(ml_dtypes.float4_e2m1fn).view(np.uint8) & 0xF
        words = c[..., 0::2] | (c[..., 1::2] << 4)
    return np.ascontiguousarray(words), np.ascontiguousarray(byte.astype(np.uint8).reshape(k // 512, 16, n))


def unpack_weight(words, scales, fmt):
    g, p, n, _ = words.shape
    if fmt == "e4m3":
        vals = np.ascontiguousarray(words).view(ml_dtypes.float8_e4m3fn).astype(np.float64)
    else:
        nib = np.empty((g, p, n, 4), np.uint8)
        nib[..., 0::2] = words & 0xF
        nib[..., 1::2] = words >> 4
        vals = E2M1[nib]
    vals = vals * np.repeat(np.exp2(scales.astype(np.float64) - 127.0), 8, axis=1)[..., None]
    return vals.transpose(0, 1, 3, 2).reshape(g * 512, n)
def pack4(w):
    words, scales = pack_weight(w, "e2m1")
    return words.reshape(words.shape[0], 128, -1), scales


def unpack4(words, scales):
    return unpack_weight(words.reshape(words.shape[0], 128, -1, 2), scales, "e2m1")


def planes(Y):
    n, m = Y.shape
    b = f64(bf(Y)).reshape(n // 32, 32, m)
    amax = np.abs(b).max(1)
    byte = np.clip(np.where(amax > 0, np.frexp(amax)[1] - 1 + 127 - 7, 1), 1, 254)
    codes = (b * np.exp2(127.0 - byte)[:, None, :]).reshape(n, m).astype(np.float32).astype(ml_dtypes.float8_e4m3fn).view(np.uint8)
    words = codes.reshape(n // 512, 128, 4, m).transpose(0, 1, 3, 2)
    return np.ascontiguousarray(words), np.ascontiguousarray(byte.astype(np.uint8).reshape(n // 512, 16, m))


V, N, P, D = 512, 2048, 1536, 2560
COMMON = 0.16

def setup_inputs():
    s = mx_kscale(P)
    t = mx_kscale(N)
    common = np.random.randn(P, 1)
    tr = np.random.randn(P, N) + COMMON * common
    va = (np.random.randn(P, V) + COMMON * common) / np.sqrt(P)
    train_words, train_scales = pack4(tr * s[:, None] * t[None, :])
    val_words, val_scales = pack4(va / s[:, None])
    spread = np.exp(0.8 * np.random.randn(D))
    return {
        "train_words": train_words, "train_scales": train_scales,
        "val_words": val_words, "val_scales": val_scales,
        "offset": bf(0.5 * np.random.randn(N) * t),
        "grad": bf(np.random.randn(N, D) * spread[None, :] / np.sqrt(N) / t[:, None]),
        "mass": bf(np.exp(0.3 * np.random.randn(V))),
        "decay": bf(0.6 + 0.1 * np.random.randn(D)),
        "mom": bf(np.random.randn(V, D) * spread[None, :]),
    }

def reference(train_words, train_scales, val_words, val_scales, offset, grad, mass, decay, mom):
    A = unpack4(train_words, train_scales)
    B = unpack4(val_words, val_scales)
    S = A.T @ B
    R = np.maximum(S + f64(offset)[:, None], 0.0)
    U = mxq(R, 0).T @ mxq(f64(grad), 0)
    y = U / f64(mass)[:, None] + f64(decay)[None, :] * f64(mom)
    words, scales = planes(y.T)
    return y, words, scales

@@ -1,0 +1,355 @@
+from contextlib import ExitStack
+
+import concourse.mybir as mybir
+from concourse.masks import make_identity
+
+V, N, K1, D = 512, 2048, 1536, 2560
+FLOPS = 2 * K1 * N * V + 2 * N * V * D
+
+F32 = mybir.dt.float32
+BF16 = mybir.dt.bfloat16
+I32 = mybir.dt.int32
+U8 = mybir.dt.uint8
+FP8X4 = mybir.dt.float8_e4m3fn_x4
+FP4X4 = mybir.dt.float4_e2m1fn_x4
+ALU = mybir.AluOpType
+ACT = mybir.ActivationFunctionType
+
+P = 128
+PACK = 4
+W = 512
+K1_PASSES = K1 // W
+N_PASSES = N // W
+CHUNKS = D // W
+V_TILES = V // P
+TILES = CHUNKS * N_PASSES
+HEAD_TILES = 2 * N_PASSES
+STEP_TILES = 3
+VECTOR_COLS_HEAD = 232
+VECTOR_COLS = 144
+
+def tile_relu_alignment_reweighted_gradients_k5_kernel(
+    tc, train_words, train_scales, val_words, val_scales, offset, grad, mass, decay, mom, out_0, out_1, out_2
+):
+    nc = tc.nc
+    with ExitStack() as ctx:
+        keep = ctx.enter_context(tc.tile_pool(name="keep", bufs=1))
+        work = ctx.enter_context(tc.tile_pool(name="work", bufs=2))
+        psum = ctx.enter_context(tc.psum_pool(name="psum", bufs=1))
+        ctx.enter_context(tc.manual_schedule())
+
+        ident_bf = keep.tile([P, P], BF16, name="ident_bf")
+        ident_f32 = keep.tile([P, P], F32, name="ident_f32")
+        offset_rows = keep.tile([N_PASSES, W], BF16, name="offset_rows")
+        blocks = (PACK, CHUNKS + 1)
+        rows = [keep.tile([P, blocks[i], P], BF16, name="rows%d" % i) for i in range(2)]
+        cols = [keep.tile([P, blocks[i], 4], BF16, name="cols%d" % i) for i in range(2)]
+        inv_mass = keep.tile([P, V_TILES], F32, name="inv_mass")
+        b_words = keep.tile([P, K1_PASSES, 2 * V], U8, name="b_words", align_bytes=64)
+        b_scales = keep.tile([P, K1_PASSES, V], U8, name="b_scales", align_bytes=64)
+        a_scales_raw = keep.tile([P, K1_PASSES, N], U8, name="a_scales_raw")
+        a_words_raw = [keep.tile([P, K1_PASSES, 2 * W], U8, name="a_words_raw%d" % g) for g in range(N_PASSES)]
+        r_codes = keep.tile([P, N_PASSES, V], I32, name="r_codes", align_bytes=64)
+        r_scales = keep.tile([P, N_PASSES, V], U8, name="r_scales", align_bytes=64)
+        y_scales = keep.tile([P, CHUNKS, V], U8, name="y_scales", align_bytes=64)
+
+        order = [(c, g) for g in range(N_PASSES) for c in range(2)]
+        order += [(c, g) for c in range(2, CHUNKS) for g in range(N_PASSES)]
+        a_words, a_scales, r_rows, r_grouped = {}, {}, {}, {}
+        g_raw, g_grouped, g_codes, g_scales = {}, {}, {}, {}
+        mom_sb, decay_ps, y, y_bf, y_t, y_grouped, y_codes, u_ps = {}, {}, {}, {}, {}, {}, {}, {}
+
+        def load_scale_rows(queue, plane, scales, rows_of_four):
+            by_row = scales.rearrange("k (q r) n -> r q k n", r=4)
+            for r in rows_of_four:
+                queue.dma_start(out=plane[r:P:32, :, :].bitcast(I32), in_=by_row[r].bitcast(I32))
+
+        def load_a_words(g):
+            src = train_words[:, :, 2 * W * g : 2 * W * (g + 1)].rearrange("k p b -> p k b")
+            nc.sync.dma_start(out=a_words_raw[g][:].bitcast(I32), in_=src.bitcast(I32))
+
+        def load_grad(c, g, chunks):
+            raw = work.tile([P, PACK, W * chunks], BF16, name="g_raw", tag="g_raw", bufs=8)
+            src = grad[W * g : W * (g + 1), W * c : W * (c + chunks)].rearrange("(j t e) d -> e j t d", t=PACK, e=4)
+            for e in range(4):
+                nc.sync.dma_start(out=raw[e:P:4, :, :], in_=src[e])
+            for i in range(chunks):
+                g_raw[c + i, g] = raw[:, :, W * i : W * (i + 1)]
+
+        def load_mom(c):
+            mom_sb[c] = work.tile([P, V_TILES, W], BF16, name="mom_sb", tag="mom_sb", bufs=3)
+            nc.sync.dma_start(out=mom_sb[c][:], in_=mom[:, W * c : W * (c + 1)].rearrange("(a p) d -> p a d", p=P))
+
+        def interleave(copy, grouped, raw, lo, hi):
+            copy(
+                out=grouped[:, lo:hi, :].rearrange("p (c i) t -> p c t i", i=4),
+                in_=raw[:, :, lo:hi].rearrange("p t (c i) -> p c t i", i=4),
+            )
+
+        def grouped_tile():
+            return work.tile([P, W, PACK], BF16, name="grouped", tag="grouped", bufs=6, align_bytes=64)
+
+        def quantize(codes, scales, grouped):
+            nc.vector.quantize_mx(out=codes.bitcast(FP8X4), scales=scales, in_=grouped.rearrange("p w t -> p (w t)"))
+
+        def permute_a(g):
+            a_scales[g] = work.tile([P, K1_PASSES, W], U8, name="a_scales", tag="a_scales", align_bytes=64)
+            raw = a_scales_raw[:, :, W * g : W * (g + 1)]
+            nc.vector.tensor_copy(
+                out=a_scales[g][:].bitcast(I32).rearrange("p k (t j) -> p k t j", t=PACK),
+                in_=raw.bitcast(I32).rearrange("p k (j t) -> p k t j", t=PACK),
+            )
+            a_words[g] = work.tile([P, K1_PASSES, 2 * W], U8, name="a_words", tag="a_words", align_bytes=64)
+            nc.vector.tensor_copy(
+                out=a_words[g][:].bitcast(I32).rearrange("p k (t j h) -> p k t j h", t=PACK, h=2),
+                in_=a_words_raw[g][:].bitcast(I32).rearrange("p k (j t h) -> p k t j h", t=PACK, h=2),
+            )
+
+        def alignment(g, t):
+            if t == 0:
+                r_rows[g] = work.tile([P, PACK, V], BF16, name="r_rows", tag="r_rows")
+            s_ps = psum.tile([P, V], F32, name="s_ps", tag="aux", bufs=3)
+            for k in range(K1_PASSES):
+                nc.tensor.matmul_mx(
+                    out=s_ps[:],
+                    lhsT=a_words[g][:, k, 2 * P * t : 2 * P * (t + 1)].bitcast(FP4X4),
+                    lhsT_scale=a_scales[g][:, k, P * t : P * (t + 1)],
+                    rhs=b_words[:, k, :].bitcast(FP4X4),
+                    rhs_scale=b_scales[:, k, :],
+                    start=(k == 0),
+                    stop=(k == K1_PASSES - 1),
+                )
+            nc.scalar.activation(out=r_rows[g][:, t, :], in_=s_ps[:], func=ACT.Relu, bias=cols[0][:, t, g : g + 1])
+
+        def interleave_r(g):
+            r_grouped[g] = grouped_tile()
+            interleave(nc.vector.tensor_copy, r_grouped[g], r_rows[g], 0, V)
+
+        def quantize_r(g):
+            quantize(r_codes[:, g, :], r_scales[:, g, :], r_grouped[g][:])
+
+        def split(i):
+            return VECTOR_COLS_HEAD if i < HEAD_TILES else VECTOR_COLS
+
+        def interleave_g_scalar(i):
+            g_grouped[i] = grouped_tile()
+            interleave(nc.scalar.copy, g_grouped[i], g_raw[order[i]], split(i), W)
+
+        def interleave_g_vector(i):
+            interleave(nc.vector.tensor_copy, g_grouped[i], g_raw[order[i]], 0, split(i))
+
+        def quantize_g(i):
+            g_codes[order[i]] = work.tile([P, W], I32, name="g_codes", tag="g_codes", bufs=8, align_bytes=64)
+            g_scales[order[i]] = work.tile([P, W], U8, name="g_scales", tag="g_scales", bufs=8, align_bytes=64)
+            quantize(g_codes[order[i]][:], g_scales[order[i]][:], g_grouped[i][:])
+
+        def weighted_sum_pass(c, g):
+            for a in range(V_TILES):
+                if g == 0:
+                    u_ps[c, a] = psum.tile([P, W], F32, name="u_ps", tag="u_ps", bufs=4)
+                nc.tensor.matmul_mx(
+                    out=u_ps[c, a][:],
+                    lhsT=r_codes[:, g, P * a : P * (a + 1)].bitcast(FP8X4),
+                    lhsT_scale=r_scales[:, g, P * a : P * (a + 1)],
+                    rhs=g_codes[c, g][:].bitcast(FP8X4),
+                    rhs_scale=g_scales[c, g][:],
+                    start=(g == 0),
+                    stop=(g == N_PASSES - 1),
+                )
+
+        def spread_decay(c):
+            decay_ps[c] = psum.tile([P, W], BF16, name="decay_ps", tag="decay_ps")
+            for s in range(PACK):
+                row, block = divmod(PACK * c + s, CHUNKS)
+                column = cols[1][:, block, row : row + 1].to_broadcast([P, P])
+                nc.tensor.transpose(decay_ps[c][:, P * s : P * (s + 1)], column, ident_bf[:])
+
+        def decayed_momentum(c, half):
+            if half == 0:
+                y[c] = work.tile([P, V_TILES, W], F32, name="y", tag="y", bufs=3)
+            tiles = slice(2 * half, 2 * half + 2)
+            nc.vector.tensor_tensor(
+                out=y[c][:, tiles, :],
+                in0=decay_ps[c][:].unsqueeze(1).to_broadcast([P, 2, W]),
+                in1=mom_sb[c][:, tiles, :],
+                op=ALU.mult,
+            )
+
+        def combine(c, a):
+            nc.vector.scalar_tensor_tensor(
+                out=y[c][:, a, :],
+                in0=u_ps[c, a][:],
+                scalar=inv_mass[:, a : a + 1],
+                in1=y[c][:, a, :],
+                op0=ALU.mult,
+                op1=ALU.add,
+            )
+
+        def store_y(c, lo, hi):
+            dst = out_0[:, W * c : W * (c + 1)].rearrange("(a p) d -> p a d", p=P)
+            nc.sync.dma_start(out=dst[:, lo:hi, :], in_=y[c][:, lo:hi, :])
+
+        def round_y(c, a):
+            if a == 0:
+                y_bf[c] = work.tile([P, V_TILES, W], BF16, name="y_bf", tag="y_bf")
+            dst = y_bf[c][:, a, :].rearrange("p (u m e) -> p u m e", u=2, e=2)
+            src = y[c][:, a, :].rearrange("p (m u e) -> p u m e", u=2, e=2)
+            nc.scalar.copy(out=dst, in_=src)
+
+        def transpose_y(c, lo, hi):
+            y_t[c, lo] = psum.tile([P, hi - lo, 2, P], F32, name="y_t", tag="aux", bufs=3)
+            for a in range(lo, hi):
+                pairs = y_bf[c][:, a, :].bitcast(F32)
+                for u in range(2):
+                    nc.tensor.transpose(y_t[c, lo][:, a - lo, u, :], pairs[:, P * u : P * (u + 1)], ident_f32[:])
+
+        def group_y(copy, c, lo, hi):
+            if lo == 0:
+                y_grouped[c] = work.tile([P, V, PACK], BF16, name="y_grouped", tag="y_grouped", align_bytes=64)
+            dst = y_grouped[c][:, P * lo : P * hi, :].bitcast(F32)
+            copy(out=dst.rearrange("p (a v) u -> p a v u", v=P), in_=y_t[c, lo][:].rearrange("p a u v -> p a v u"))
+
+        def quantize_y(c, lo, hi):
+            if lo == 0:
+                y_codes[c] = work.tile([P, V], I32, name="y_codes", tag="y_codes", align_bytes=64)
+            span = slice(P * lo, P * hi)
+            quantize(y_codes[c][:, span], y_scales[:, c, span], y_grouped[c][:, span, :])
+            dst = out_1[c].rearrange("p m t -> p (m t)").bitcast(I32)
+            nc.sync.dma_start(out=dst[:, span], in_=y_codes[c][:, span])
+
+        def store_y_scales(lo, hi):
+            for q in range(4):
+                dst = out_2[lo:hi, 4 * q : 4 * q + 4, :].rearrange("c r m -> r c m")
+                nc.sync.dma_start(out=dst.bitcast(I32), in_=y_scales[32 * q : 32 * q + 4, lo:hi, :].bitcast(I32))
+
+        def turn_rows(i):
+            rows_t = psum.tile([P, blocks[i], P], BF16, name="rows_t", tag="aux", bufs=3)
+            for s in range(blocks[i]):
+                nc.tensor.transpose(rows_t[:, s, :], rows[i][:, s, :], ident_bf[:])
+            nc.scalar.copy(out=cols[i][:], in_=rows_t[:, :, 0:4])
+
+        nc.vector.memset(b_scales[:].bitcast(I32), 0)
+        nc.vector.memset(a_scales_raw[:].bitcast(I32), 0)
+        nc.vector.memset(rows[0][:].bitcast(I32), 0)
+        nc.vector.memset(rows[1][:].bitcast(I32), 0)
+        nc.scalar.dma_start(out=offset_rows[:], in_=offset.rearrange("(g n) -> g n", n=W))
+        load_scale_rows(nc.gpsimd, b_scales, val_scales, range(2))
+        make_identity(nc, ident_bf[:])
+        nc.scalar.activation(out=ident_f32[:], in_=ident_bf[:], func=ACT.Relu)
+        nc.sync.dma_start(out=b_words[:].bitcast(I32), in_=val_words.rearrange("k p b -> p k b").bitcast(I32))
+        load_a_words(0)
+        load_scale_rows(nc.sync, a_scales_raw, train_scales, range(4))
+        load_scale_rows(nc.sync, b_scales, val_scales, range(2, 4))
+        load_grad(0, 0, 2)
+        load_a_words(1)
+        for g in range(1, N_PASSES):
+            load_grad(0, g, 2)
+            if g + 1 < N_PASSES:
+                load_a_words(g + 1)
+            if g == 1:
+                nc.sync.dma_start(out=rows[1][0:4, 0:CHUNKS, :], in_=decay.rearrange("(r b d) -> r b d", r=4, d=P))
+                nc.sync.dma_start(out=rows[1][0:4, CHUNKS, :], in_=mass.rearrange("(a p) -> a p", p=P))
+            if g == 2:
+                load_mom(0)
+        load_grad(2, 0, 2)
+        load_mom(1)
+        for g in range(1, N_PASSES):
+            load_grad(2, g, 2)
+
+        nc.vector.tensor_copy(
+            out=rows[0][0:N_PASSES, :, :].rearrange("g t (j e) -> g t j e", e=4),
+            in_=offset_rows[:].rearrange("g (j t e) -> g t j e", t=PACK, e=4),
+        )
+        turn_rows(0)
+        permute_a(0)
+
+        for g in range(N_PASSES):
+            interleave_g_scalar(2 * g)
+            interleave_g_vector(2 * g)
+            if g > 0:
+                interleave_r(g - 1)
+                quantize_g(2 * g - 1)
+            if 0 < g < N_PASSES - 1:
+                permute_a(g + 1)
+            if g > 0:
+                quantize_r(g - 1)
+            alignment(g, 0)
+            alignment(g, 1)
+            interleave_g_scalar(2 * g + 1)
+            interleave_g_vector(2 * g + 1)
+            quantize_g(2 * g)
+            if g == 0:
+                permute_a(1)
+            alignment(g, 2)
+            alignment(g, 3)
+            if g > 0:
+                weighted_sum_pass(0, g - 1)
+            if g == 1:
+                turn_rows(1)
+            if g == 2:
+                spread_decay(0)
+        nc.vector.reciprocal(out=inv_mass[:], in_=cols[1][:, CHUNKS, :])
+        decayed_momentum(0, 0)
+        interleave_r(N_PASSES - 1)
+        quantize_g(HEAD_TILES - 1)
+        interleave_g_scalar(HEAD_TILES)
+        quantize_r(N_PASSES - 1)
+        weighted_sum_pass(0, N_PASSES - 1)
+        decayed_momentum(0, 1)
+        spread_decay(1)
+        interleave_g_vector(HEAD_TILES)
+        load_mom(2)
+        for g in range(N_PASSES):
+            load_grad(CHUNKS - 1, g, 1)
+
+        for c in range(CHUNKS - 1):
+            first = HEAD_TILES + STEP_TILES * c
+            ready = min(2, first - N_PASSES * (c + 1))
+            interleave_g_scalar(first + 1)
+            for a in range(V_TILES):
+                combine(c, a)
+            for g in range(ready):
+                weighted_sum_pass(c + 1, g)
+            for a in range(V_TILES):
+                round_y(c, a)
+            decayed_momentum(c + 1, 0)
+            decayed_momentum(c + 1, 1)
+            store_y(c, 0, V_TILES)
+            if c + 3 < CHUNKS:
+                load_mom(c + 3)
+            transpose_y(c, 0, 2)
+            transpose_y(c, 2, 4)
+            if c + 2 < CHUNKS:
+                spread_decay(c + 2)
+            done = ready
+            for i in range(first, first + STEP_TILES):
+                if i + 1 < TILES:
+                    if i > first:
+                        interleave_g_scalar(i + 1)
+                    interleave_g_vector(i + 1)
+                if i == first + 1:
+                    group_y(nc.scalar.copy, c, 0, 2)
+                    group_y(nc.scalar.copy, c, 2, 4)
+                if i == first + 2 and i + 1 < TILES:
+                    quantize_y(c, 0, V_TILES)
+                quantize_g(i)
+                while done < N_PASSES and N_PASSES * (c + 1) + done <= i:
+                    weighted_sum_pass(c + 1, done)
+                    done += 1
+        last = CHUNKS - 1
+        quantize_y(last - 1, 0, V_TILES)
+        store_y_scales(0, last)
+        for a in range(V_TILES):
+            combine(last, a)
+            round_y(last, a)
+            if a % 2 == 1:
+                store_y(last, a - 1, a + 1)
+        transpose_y(last, 0, 2)
+        transpose_y(last, 2, 3)
+        transpose_y(last, 3, 4)
+        group_y(nc.vector.tensor_copy, last, 0, 2)
+        group_y(nc.vector.tensor_copy, last, 2, 3)
+        quantize_y(last, 0, 2)
+        group_y(nc.vector.tensor_copy, last, 3, 4)
+        quantize_y(last, 2, 4)
+        store_y_scales(last, CHUNKS)

@@ -25,7 +25,7 @@ V_TILES = V // P
 TILES = CHUNKS * N_PASSES
 HEAD_TILES = 2 * N_PASSES
 STEP_TILES = 3
-VECTOR_COLS_HEAD = 232
+VECTOR_COLS_HEAD = 72
 VECTOR_COLS = 144
 
 def tile_relu_alignment_reweighted_gradients_k5_kernel(
@@ -40,24 +40,24 @@ def tile_relu_alignment_reweighted_gradients_k5_kernel(
 
         ident_bf = keep.tile([P, P], BF16, name="ident_bf")
         ident_f32 = keep.tile([P, P], F32, name="ident_f32")
-        offset_rows = keep.tile([N_PASSES, W], BF16, name="offset_rows")
-        blocks = (PACK, CHUNKS + 1)
-        rows = [keep.tile([P, blocks[i], P], BF16, name="rows%d" % i) for i in range(2)]
-        cols = [keep.tile([P, blocks[i], 4], BF16, name="cols%d" % i) for i in range(2)]
+        offset_cols = keep.tile([P, N // P], BF16, name="offset_cols")
+        rows = keep.tile([P, CHUNKS + 1, P], BF16, name="rows")
+        cols = keep.tile([P, CHUNKS + 1, 4], BF16, name="cols")
         inv_mass = keep.tile([P, V_TILES], F32, name="inv_mass")
         b_words = keep.tile([P, K1_PASSES, 2 * V], U8, name="b_words", align_bytes=64)
         b_scales = keep.tile([P, K1_PASSES, V], U8, name="b_scales", align_bytes=64)
-        a_scales_raw = keep.tile([P, K1_PASSES, N], U8, name="a_scales_raw")
-        a_words_raw = [keep.tile([P, K1_PASSES, 2 * W], U8, name="a_words_raw%d" % g) for g in range(N_PASSES)]
+        a_scales = keep.tile([P, K1_PASSES, N], U8, name="a_scales", align_bytes=64)
+        a_words = [keep.tile([P, K1_PASSES, 2 * W], U8, name="a_words%d" % g, align_bytes=64) for g in range(N_PASSES)]
+        offset_all = keep.tile([P, N], BF16, name="offset_all")
         r_codes = keep.tile([P, N_PASSES, V], I32, name="r_codes", align_bytes=64)
         r_scales = keep.tile([P, N_PASSES, V], U8, name="r_scales", align_bytes=64)
         y_scales = keep.tile([P, CHUNKS, V], U8, name="y_scales", align_bytes=64)
 
         order = [(c, g) for g in range(N_PASSES) for c in range(2)]
         order += [(c, g) for c in range(2, CHUNKS) for g in range(N_PASSES)]
-        a_words, a_scales, r_rows, r_grouped = {}, {}, {}, {}
+        z_bf, r_grouped, turned = {}, {}, {}
         g_raw, g_grouped, g_codes, g_scales = {}, {}, {}, {}
-        mom_sb, decay_ps, y, y_bf, y_t, y_grouped, y_codes, u_ps = {}, {}, {}, {}, {}, {}, {}, {}
+        mom_sb, decay_ps, y, y_bf, y_grouped, y_codes, u_ps = {}, {}, {}, {}, {}, {}, {}
 
         def load_scale_rows(queue, plane, scales, rows_of_four):
             by_row = scales.rearrange("k (q r) n -> r q k n", r=4)
@@ -66,13 +66,12 @@ def tile_relu_alignment_reweighted_gradients_k5_kernel(
 
         def load_a_words(g):
             src = train_words[:, :, 2 * W * g : 2 * W * (g + 1)].rearrange("k p b -> p k b")
-            nc.sync.dma_start(out=a_words_raw[g][:].bitcast(I32), in_=src.bitcast(I32))
+            nc.sync.dma_start(out=a_words[g][:].bitcast(I32), in_=src.bitcast(I32))
 
         def load_grad(c, g, chunks):
             raw = work.tile([P, PACK, W * chunks], BF16, name="g_raw", tag="g_raw", bufs=8)
-            src = grad[W * g : W * (g + 1), W * c : W * (c + chunks)].rearrange("(j t e) d -> e j t d", t=PACK, e=4)
-            for e in range(4):
-                nc.sync.dma_start(out=raw[e:P:4, :, :], in_=src[e])
+            src = grad[W * g : W * (g + 1), W * c : W * (c + chunks)].rearrange("(p t) d -> p t d", t=PACK)
+            nc.sync.dma_start(out=raw[:], in_=src)
             for i in range(chunks):
                 g_raw[c + i, g] = raw[:, :, W * i : W * (i + 1)]
 
@@ -92,38 +91,64 @@ def tile_relu_alignment_reweighted_gradients_k5_kernel(
         def quantize(codes, scales, grouped):
             nc.vector.quantize_mx(out=codes.bitcast(FP8X4), scales=scales, in_=grouped.rearrange("p w t -> p (w t)"))
 
-        def permute_a(g):
-            a_scales[g] = work.tile([P, K1_PASSES, W], U8, name="a_scales", tag="a_scales", align_bytes=64)
-            raw = a_scales_raw[:, :, W * g : W * (g + 1)]
-            nc.vector.tensor_copy(
-                out=a_scales[g][:].bitcast(I32).rearrange("p k (t j) -> p k t j", t=PACK),
-                in_=raw.bitcast(I32).rearrange("p k (j t) -> p k t j", t=PACK),
-            )
-            a_words[g] = work.tile([P, K1_PASSES, 2 * W], U8, name="a_words", tag="a_words", align_bytes=64)
-            nc.vector.tensor_copy(
-                out=a_words[g][:].bitcast(I32).rearrange("p k (t j h) -> p k t j h", t=PACK, h=2),
-                in_=a_words_raw[g][:].bitcast(I32).rearrange("p k (j t h) -> p k t j h", t=PACK, h=2),
-            )
+        def pair_order(ap):
+            return ap.rearrange("p (m u e) -> p u m e", u=2, e=2)
 
-        def alignment(g, t):
-            if t == 0:
-                r_rows[g] = work.tile([P, PACK, V], BF16, name="r_rows", tag="r_rows")
-            s_ps = psum.tile([P, V], F32, name="s_ps", tag="aux", bufs=3)
+        def pair_major(ap):
+            return ap.rearrange("p (u m e) -> p u m e", u=2, e=2)
+
+        def rounded_tile():
+            return work.tile([P, V_TILES, W], BF16, name="rounded", tag="rounded", bufs=3)
+
+        def turn(key, rounded, lo, hi):
+            turned[key, lo] = psum.tile([P, hi - lo, 2, P], F32, name="turned", tag="turned", bufs=2)
+            for a in range(lo, hi):
+                pairs = rounded[:, a, :].bitcast(F32)
+                for u in range(2):
+                    nc.tensor.transpose(turned[key, lo][:, a - lo, u, :], pairs[:, P * u : P * (u + 1)], ident_f32[:])
+
+        def group(copy, key, grouped, lo, hi):
+            dst = grouped[:, P * lo : P * hi, :].bitcast(F32)
+            copy(out=dst.rearrange("p (a v) u -> p a v u", v=P), in_=turned[key, lo][:].rearrange("p a u v -> p a v u"))
+
+        def spread_offset(half):
+            spread = psum.tile([P, 4, P], F32, name="spread", tag="turned", bufs=2)
+            for s in range(4):
+                column = offset_cols[:].bitcast(F32)[:, 4 * half + s : 4 * half + s + 1].to_broadcast([P, P])
+                nc.tensor.transpose(spread[:, s, :], column, ident_f32[:])
+            dst = offset_all[:].bitcast(F32).rearrange("p (k s) -> p k s", s=8)[:, :, 4 * half : 4 * half + 4]
+            nc.scalar.copy(out=dst, in_=spread[:].rearrange("p s k -> p k s"))
+
+        def alignment(g, a):
+            if a == 0:
+                z_bf[g] = rounded_tile()
+            s_ps = psum.tile([P, W], F32, name="s_ps", tag="acc", bufs=5)
             for k in range(K1_PASSES):
                 nc.tensor.matmul_mx(
                     out=s_ps[:],
-                    lhsT=a_words[g][:, k, 2 * P * t : 2 * P * (t + 1)].bitcast(FP4X4),
-                    lhsT_scale=a_scales[g][:, k, P * t : P * (t + 1)],
-                    rhs=b_words[:, k, :].bitcast(FP4X4),
-                    rhs_scale=b_scales[:, k, :],
+                    lhsT=b_words[:, k, 2 * P * a : 2 * P * (a + 1)].bitcast(FP4X4),
+                    lhsT_scale=b_scales[:, k, P * a : P * (a + 1)],
+                    rhs=a_words[g][:, k, :].bitcast(FP4X4),
+                    rhs_scale=a_scales[:, k, W * g : W * (g + 1)],
                     start=(k == 0),
                     stop=(k == K1_PASSES - 1),
                 )
-            nc.scalar.activation(out=r_rows[g][:, t, :], in_=s_ps[:], func=ACT.Relu, bias=cols[0][:, t, g : g + 1])
+            nc.vector.tensor_tensor(
+                out=pair_major(z_bf[g][:, a, :]),
+                in0=pair_order(s_ps[:]),
+                in1=pair_order(offset_all[:, W * g : W * (g + 1)]),
+                op=ALU.add,
+            )
 
-        def interleave_r(g):
+        def turn_r(g):
             r_grouped[g] = grouped_tile()
-            interleave(nc.vector.tensor_copy, r_grouped[g], r_rows[g], 0, V)
+            for lo in (0, 2):
+                turn(("r", g), z_bf[g], lo, lo + 2)
+                group(nc.scalar.copy, ("r", g), r_grouped[g], lo, lo + 2)
+
+        def relu_r(g):
+            flat = r_grouped[g][:].rearrange("p w t -> p (w t)")
+            nc.vector.tensor_scalar(out=flat, in0=flat, scalar1=0.0, scalar2=None, op0=ALU.max)
 
         def quantize_r(g):
             quantize(r_codes[:, g, :], r_scales[:, g, :], r_grouped[g][:])
@@ -146,7 +171,7 @@ def tile_relu_alignment_reweighted_gradients_k5_kernel(
         def weighted_sum_pass(c, g):
             for a in range(V_TILES):
                 if g == 0:
-                    u_ps[c, a] = psum.tile([P, W], F32, name="u_ps", tag="u_ps", bufs=4)
+                    u_ps[c, a] = psum.tile([P, W], F32, name="u_ps", tag="acc", bufs=5)
                 nc.tensor.matmul_mx(
                     out=u_ps[c, a][:],
                     lhsT=r_codes[:, g, P * a : P * (a + 1)].bitcast(FP8X4),
@@ -161,7 +186,7 @@ def tile_relu_alignment_reweighted_gradients_k5_kernel(
             decay_ps[c] = psum.tile([P, W], BF16, name="decay_ps", tag="decay_ps")
             for s in range(PACK):
                 row, block = divmod(PACK * c + s, CHUNKS)
-                column = cols[1][:, block, row : row + 1].to_broadcast([P, P])
+                column = cols[:, block, row : row + 1].to_broadcast([P, P])
                 nc.tensor.transpose(decay_ps[c][:, P * s : P * (s + 1)], column, ident_bf[:])
 
         def decayed_momentum(c, half):
@@ -191,23 +216,17 @@ def tile_relu_alignment_reweighted_gradients_k5_kernel(
 
         def round_y(c, a):
             if a == 0:
-                y_bf[c] = work.tile([P, V_TILES, W], BF16, name="y_bf", tag="y_bf")
-            dst = y_bf[c][:, a, :].rearrange("p (u m e) -> p u m e", u=2, e=2)
-            src = y[c][:, a, :].rearrange("p (m u e) -> p u m e", u=2, e=2)
+                y_bf[c] = rounded_tile()
+            dst, src = pair_major(y_bf[c][:, a, :]), pair_order(y[c][:, a, :])
             nc.scalar.copy(out=dst, in_=src)
 
         def transpose_y(c, lo, hi):
-            y_t[c, lo] = psum.tile([P, hi - lo, 2, P], F32, name="y_t", tag="aux", bufs=3)
-            for a in range(lo, hi):
-                pairs = y_bf[c][:, a, :].bitcast(F32)
-                for u in range(2):
-                    nc.tensor.transpose(y_t[c, lo][:, a - lo, u, :], pairs[:, P * u : P * (u + 1)], ident_f32[:])
+            turn(("y", c), y_bf[c], lo, hi)
 
         def group_y(copy, c, lo, hi):
             if lo == 0:
                 y_grouped[c] = work.tile([P, V, PACK], BF16, name="y_grouped", tag="y_grouped", align_bytes=64)
-            dst = y_grouped[c][:, P * lo : P * hi, :].bitcast(F32)
-            copy(out=dst.rearrange("p (a v) u -> p a v u", v=P), in_=y_t[c, lo][:].rearrange("p a u v -> p a v u"))
+            group(copy, ("y", c), y_grouped[c], lo, hi)
 
         def quantize_y(c, lo, hi):
             if lo == 0:
@@ -217,38 +236,34 @@ def tile_relu_alignment_reweighted_gradients_k5_kernel(
             dst = out_1[c].rearrange("p m t -> p (m t)").bitcast(I32)
             nc.sync.dma_start(out=dst[:, span], in_=y_codes[c][:, span])
 
-        def store_y_scales(lo, hi):
+        def store_y_scales(queue, lo, hi):
             for q in range(4):
                 dst = out_2[lo:hi, 4 * q : 4 * q + 4, :].rearrange("c r m -> r c m")
-                nc.sync.dma_start(out=dst.bitcast(I32), in_=y_scales[32 * q : 32 * q + 4, lo:hi, :].bitcast(I32))
+                queue.dma_start(out=dst.bitcast(I32), in_=y_scales[32 * q : 32 * q + 4, lo:hi, :].bitcast(I32))
 
-        def turn_rows(i):
-            rows_t = psum.tile([P, blocks[i], P], BF16, name="rows_t", tag="aux", bufs=3)
-            for s in range(blocks[i]):
-                nc.tensor.transpose(rows_t[:, s, :], rows[i][:, s, :], ident_bf[:])
-            nc.scalar.copy(out=cols[i][:], in_=rows_t[:, :, 0:4])
+        def turn_rows():
+            rows_t = psum.tile([P, CHUNKS + 1, P], BF16, name="rows_t", tag="decay_ps")
+            for s in range(CHUNKS + 1):
+                nc.tensor.transpose(rows_t[:, s, :], rows[:, s, :], ident_bf[:])
+            nc.scalar.copy(out=cols[:], in_=rows_t[:, :, 0:4])
 
+        nc.scalar.dma_start(out=offset_cols[:], in_=offset.rearrange("(p s) -> p s", p=P))
+        make_identity(nc, ident_f32[:])
         nc.vector.memset(b_scales[:].bitcast(I32), 0)
-        nc.vector.memset(a_scales_raw[:].bitcast(I32), 0)
-        nc.vector.memset(rows[0][:].bitcast(I32), 0)
-        nc.vector.memset(rows[1][:].bitcast(I32), 0)
-        nc.scalar.dma_start(out=offset_rows[:], in_=offset.rearrange("(g n) -> g n", n=W))
-        load_scale_rows(nc.gpsimd, b_scales, val_scales, range(2))
-        make_identity(nc, ident_bf[:])
-        nc.scalar.activation(out=ident_f32[:], in_=ident_bf[:], func=ACT.Relu)
+        nc.vector.memset(a_scales[:].bitcast(I32), 0)
+        nc.vector.memset(rows[:].bitcast(I32), 0)
+        nc.scalar.copy(out=ident_bf[:], in_=ident_f32[:])
         nc.sync.dma_start(out=b_words[:].bitcast(I32), in_=val_words.rearrange("k p b -> p k b").bitcast(I32))
         load_a_words(0)
-        load_scale_rows(nc.sync, a_scales_raw, train_scales, range(4))
-        load_scale_rows(nc.sync, b_scales, val_scales, range(2, 4))
-        load_grad(0, 0, 2)
-        load_a_words(1)
-        for g in range(1, N_PASSES):
+        load_scale_rows(nc.sync, b_scales, val_scales, range(4))
+        load_scale_rows(nc.sync, a_scales, train_scales, range(4))
+        for g in range(N_PASSES):
             load_grad(0, g, 2)
             if g + 1 < N_PASSES:
                 load_a_words(g + 1)
             if g == 1:
-                nc.sync.dma_start(out=rows[1][0:4, 0:CHUNKS, :], in_=decay.rearrange("(r b d) -> r b d", r=4, d=P))
-                nc.sync.dma_start(out=rows[1][0:4, CHUNKS, :], in_=mass.rearrange("(a p) -> a p", p=P))
+                nc.sync.dma_start(out=rows[0:4, 0:CHUNKS, :], in_=decay.rearrange("(r b d) -> r b d", r=4, d=P))
+                nc.sync.dma_start(out=rows[0:4, CHUNKS, :], in_=mass.rearrange("(a p) -> a p", p=P))
             if g == 2:
                 load_mom(0)
         load_grad(2, 0, 2)
@@ -256,48 +271,46 @@ def tile_relu_alignment_reweighted_gradients_k5_kernel(
         for g in range(1, N_PASSES):
             load_grad(2, g, 2)
 
-        nc.vector.tensor_copy(
-            out=rows[0][0:N_PASSES, :, :].rearrange("g t (j e) -> g t j e", e=4),
-            in_=offset_rows[:].rearrange("g (j t e) -> g t j e", t=PACK, e=4),
-        )
-        turn_rows(0)
-        permute_a(0)
+        spread_offset(0)
+        spread_offset(1)
 
         for g in range(N_PASSES):
-            interleave_g_scalar(2 * g)
-            interleave_g_vector(2 * g)
-            if g > 0:
-                interleave_r(g - 1)
-                quantize_g(2 * g - 1)
-            if 0 < g < N_PASSES - 1:
-                permute_a(g + 1)
-            if g > 0:
-                quantize_r(g - 1)
             alignment(g, 0)
-            alignment(g, 1)
-            interleave_g_scalar(2 * g + 1)
-            interleave_g_vector(2 * g + 1)
-            quantize_g(2 * g)
-            if g == 0:
-                permute_a(1)
-            alignment(g, 2)
-            alignment(g, 3)
             if g > 0:
-                weighted_sum_pass(0, g - 1)
-            if g == 1:
-                turn_rows(1)
+                quantize_g(2 * g - 1)
+            interleave_g_scalar(2 * g)
+            alignment(g, 1)
+            if g > 0:
+                turn_r(g - 1)
+            interleave_g_vector(2 * g)
+            alignment(g, 2)
+            if g > 1:
+                quantize_r(g - 2)
+            interleave_g_scalar(2 * g + 1)
+            alignment(g, 3)
+            quantize_g(2 * g)
+            if g > 0:
+                relu_r(g - 1)
+            interleave_g_vector(2 * g + 1)
             if g == 2:
-                spread_decay(0)
-        nc.vector.reciprocal(out=inv_mass[:], in_=cols[1][:, CHUNKS, :])
-        decayed_momentum(0, 0)
-        interleave_r(N_PASSES - 1)
+                turn_rows()
+        last_pass = N_PASSES - 1
+        spread_decay(0)
+        nc.vector.reciprocal(out=inv_mass[:], in_=cols[:, CHUNKS, :])
+        quantize_r(last_pass - 1)
+        weighted_sum_pass(0, 0)
+        turn_r(last_pass)
+        weighted_sum_pass(0, 1)
+        weighted_sum_pass(0, 2)
         quantize_g(HEAD_TILES - 1)
+        decayed_momentum(0, 0)
         interleave_g_scalar(HEAD_TILES)
-        quantize_r(N_PASSES - 1)
-        weighted_sum_pass(0, N_PASSES - 1)
+        relu_r(last_pass)
+        interleave_g_vector(HEAD_TILES)
+        quantize_r(last_pass)
+        weighted_sum_pass(0, last_pass)
         decayed_momentum(0, 1)
         spread_decay(1)
-        interleave_g_vector(HEAD_TILES)
         load_mom(2)
         for g in range(N_PASSES):
             load_grad(CHUNKS - 1, g, 1)
@@ -338,7 +351,7 @@ def tile_relu_alignment_reweighted_gradients_k5_kernel(
                     done += 1
         last = CHUNKS - 1
         quantize_y(last - 1, 0, V_TILES)
-        store_y_scales(0, last)
+        store_y_scales(nc.sync, 0, last)
         for a in range(V_TILES):
             combine(last, a)
             round_y(last, a)
@@ -352,4 +365,4 @@ def tile_relu_alignment_reweighted_gradients_k5_kernel(
         quantize_y(last, 0, 2)
         group_y(nc.vector.tensor_copy, last, 3, 4)
         quantize_y(last, 2, 4)
-        store_y_scales(last, CHUNKS)
+        store_y_scales(nc.scalar, last, CHUNKS)

@@ -22,11 +22,7 @@ K1_PASSES = K1 // W
 N_PASSES = N // W
 CHUNKS = D // W
 V_TILES = V // P
-TILES = CHUNKS * N_PASSES
-HEAD_TILES = 2 * N_PASSES
-STEP_TILES = 3
-VECTOR_COLS_HEAD = 72
-VECTOR_COLS = 144
+HALF = W // 2
 
 def tile_relu_alignment_reweighted_gradients_k5_kernel(
     tc, train_words, train_scales, val_words, val_scales, offset, grad, mass, decay, mom, out_0, out_1, out_2
@@ -79,14 +75,8 @@ def tile_relu_alignment_reweighted_gradients_k5_kernel(
             mom_sb[c] = work.tile([P, V_TILES, W], BF16, name="mom_sb", tag="mom_sb", bufs=3)
             nc.sync.dma_start(out=mom_sb[c][:], in_=mom[:, W * c : W * (c + 1)].rearrange("(a p) d -> p a d", p=P))
 
-        def interleave(copy, grouped, raw, lo, hi):
-            copy(
-                out=grouped[:, lo:hi, :].rearrange("p (c i) t -> p c t i", i=4),
-                in_=raw[:, :, lo:hi].rearrange("p t (c i) -> p c t i", i=4),
-            )
-
-        def grouped_tile():
-            return work.tile([P, W, PACK], BF16, name="grouped", tag="grouped", bufs=6, align_bytes=64)
+        def grouped_tile(width):
+            return work.tile([P, width, PACK], BF16, name="grouped", tag="grouped", bufs=5, align_bytes=64)
 
         def quantize(codes, scales, grouped):
             nc.vector.quantize_mx(out=codes.bitcast(FP8X4), scales=scales, in_=grouped.rearrange("p w t -> p (w t)"))
@@ -100,8 +90,8 @@ def tile_relu_alignment_reweighted_gradients_k5_kernel(
         def rounded_tile():
             return work.tile([P, V_TILES, W], BF16, name="rounded", tag="rounded", bufs=3)
 
-        def turn(key, rounded, lo, hi):
-            turned[key, lo] = psum.tile([P, hi - lo, 2, P], F32, name="turned", tag="turned", bufs=2)
+        def turn(key, rounded, lo, hi, tag="turned", bufs=2):
+            turned[key, lo] = psum.tile([P, hi - lo, 2, P], F32, name="turned", tag=tag, bufs=bufs)
             for a in range(lo, hi):
                 pairs = rounded[:, a, :].bitcast(F32)
                 for u in range(2):
@@ -141,9 +131,12 @@ def tile_relu_alignment_reweighted_gradients_k5_kernel(
             )
 
         def turn_r(g):
-            r_grouped[g] = grouped_tile()
             for lo in (0, 2):
                 turn(("r", g), z_bf[g], lo, lo + 2)
+
+        def group_r(g):
+            r_grouped[g] = grouped_tile(V)
+            for lo in (0, 2):
                 group(nc.scalar.copy, ("r", g), r_grouped[g], lo, lo + 2)
 
         def relu_r(g):
@@ -153,20 +146,32 @@ def tile_relu_alignment_reweighted_gradients_k5_kernel(
         def quantize_r(g):
             quantize(r_codes[:, g, :], r_scales[:, g, :], r_grouped[g][:])
 
-        def split(i):
-            return VECTOR_COLS_HEAD if i < HEAD_TILES else VECTOR_COLS
+        def interleave_g(engine, i, lo, hi, tag="grouped"):
+            raw = g_raw[order[i]]
+            if engine == "gpsimd":
+                grouped = work.tile([P, hi - lo, PACK], BF16, name=tag, tag=tag, bufs=1, align_bytes=64)
+                nc.gpsimd.tensor_scalar(
+                    out=grouped[:],
+                    in0=raw[:, :, lo:hi].rearrange("p t w -> p w t"),
+                    scalar1=1.0,
+                    scalar2=0.0,
+                    op0=ALU.mult,
+                    op1=ALU.add,
+                )
+            else:
+                grouped = grouped_tile(hi - lo)
+                copy = nc.scalar.copy if engine == "scalar" else nc.vector.tensor_copy
+                copy(
+                    out=grouped[:].rearrange("p (c i) t -> p c t i", i=4),
+                    in_=raw[:, :, lo:hi].rearrange("p t (c i) -> p c t i", i=4),
+                )
+            g_grouped[i, lo] = grouped
 
-        def interleave_g_scalar(i):
-            g_grouped[i] = grouped_tile()
-            interleave(nc.scalar.copy, g_grouped[i], g_raw[order[i]], split(i), W)
-
-        def interleave_g_vector(i):
-            interleave(nc.vector.tensor_copy, g_grouped[i], g_raw[order[i]], 0, split(i))
-
-        def quantize_g(i):
-            g_codes[order[i]] = work.tile([P, W], I32, name="g_codes", tag="g_codes", bufs=8, align_bytes=64)
-            g_scales[order[i]] = work.tile([P, W], U8, name="g_scales", tag="g_scales", bufs=8, align_bytes=64)
-            quantize(g_codes[order[i]][:], g_scales[order[i]][:], g_grouped[i][:])
+        def quantize_g(i, lo, hi):
+            if order[i] not in g_codes:
+                g_codes[order[i]] = work.tile([P, W], I32, name="g_codes", tag="g_codes", bufs=9, align_bytes=64)
+                g_scales[order[i]] = work.tile([P, W], U8, name="g_scales", tag="g_scales", bufs=9, align_bytes=64)
+            quantize(g_codes[order[i]][:, lo:hi], g_scales[order[i]][:, lo:hi], g_grouped[i, lo][:])
 
         def weighted_sum_pass(c, g):
             for a in range(V_TILES):
@@ -189,14 +194,12 @@ def tile_relu_alignment_reweighted_gradients_k5_kernel(
                 column = cols[:, block, row : row + 1].to_broadcast([P, P])
                 nc.tensor.transpose(decay_ps[c][:, P * s : P * (s + 1)], column, ident_bf[:])
 
-        def decayed_momentum(c, half):
-            if half == 0:
-                y[c] = work.tile([P, V_TILES, W], F32, name="y", tag="y", bufs=3)
-            tiles = slice(2 * half, 2 * half + 2)
+        def decayed_momentum(c):
+            y[c] = work.tile([P, V_TILES, W], F32, name="y", tag="y", bufs=3)
             nc.vector.tensor_tensor(
-                out=y[c][:, tiles, :],
-                in0=decay_ps[c][:].unsqueeze(1).to_broadcast([P, 2, W]),
-                in1=mom_sb[c][:, tiles, :],
+                out=y[c][:],
+                in0=decay_ps[c][:].unsqueeze(1).to_broadcast([P, V_TILES, W]),
+                in1=mom_sb[c][:],
                 op=ALU.mult,
             )
 
@@ -275,58 +278,68 @@ def tile_relu_alignment_reweighted_gradients_k5_kernel(
         spread_offset(1)
 
         for g in range(N_PASSES):
+            interleave_g("scalar", 2 * g, 0, W)
+            interleave_g("gpsimd", 2 * g + 1, HALF, W, "lead")
             alignment(g, 0)
-            if g > 0:
-                quantize_g(2 * g - 1)
-            interleave_g_scalar(2 * g)
             alignment(g, 1)
             if g > 0:
                 turn_r(g - 1)
-            interleave_g_vector(2 * g)
+                group_r(g - 1)
             alignment(g, 2)
-            if g > 1:
-                quantize_r(g - 2)
-            interleave_g_scalar(2 * g + 1)
             alignment(g, 3)
-            quantize_g(2 * g)
-            if g > 0:
-                relu_r(g - 1)
-            interleave_g_vector(2 * g + 1)
             if g == 2:
                 turn_rows()
+            if g > 0:
+                quantize_g(2 * g - 1, 0, HALF)
+                relu_r(g - 1)
+            interleave_g("scalar", 2 * g + 1, 0, HALF)
+            quantize_g(2 * g, 0, W)
+            if g > 0:
+                quantize_r(g - 1)
+            quantize_g(2 * g + 1, HALF, W)
         last_pass = N_PASSES - 1
         spread_decay(0)
-        nc.vector.reciprocal(out=inv_mass[:], in_=cols[:, CHUNKS, :])
-        quantize_r(last_pass - 1)
         weighted_sum_pass(0, 0)
         turn_r(last_pass)
+        group_r(last_pass)
         weighted_sum_pass(0, 1)
         weighted_sum_pass(0, 2)
-        quantize_g(HEAD_TILES - 1)
-        decayed_momentum(0, 0)
-        interleave_g_scalar(HEAD_TILES)
+        interleave_g("gpsimd", 9, HALF, W, "lead")
+        interleave_g("scalar", 8, 0, W)
+        nc.vector.reciprocal(out=inv_mass[:], in_=cols[:, CHUNKS, :])
+        decayed_momentum(0)
         relu_r(last_pass)
-        interleave_g_vector(HEAD_TILES)
+        quantize_g(7, 0, HALF)
         quantize_r(last_pass)
         weighted_sum_pass(0, last_pass)
-        decayed_momentum(0, 1)
         spread_decay(1)
+        quantize_g(8, 0, W)
+        quantize_g(9, HALF, W)
         load_mom(2)
         for g in range(N_PASSES):
             load_grad(CHUNKS - 1, g, 1)
 
-        for c in range(CHUNKS - 1):
-            first = HEAD_TILES + STEP_TILES * c
-            ready = min(2, first - N_PASSES * (c + 1))
-            interleave_g_scalar(first + 1)
+        last = CHUNKS - 1
+        for c in range(last):
+            first = 10 + 3 * c
+            full = c + 1 < last
+            if full:
+                interleave_g("gpsimd", first, 0, W, "lead")
+                interleave_g("gpsimd", first + 2, HALF, W, "second")
+            else:
+                interleave_g("gpsimd", first, HALF, W, "lead")
+            interleave_g("scalar", first - 1, 0, HALF)
+            if c > 0:
+                group_y(nc.scalar.copy, c - 1, 0, 2)
+                group_y(nc.scalar.copy, c - 1, 2, 4)
             for a in range(V_TILES):
                 combine(c, a)
-            for g in range(ready):
+            ready = [g for g in range(N_PASSES) if N_PASSES * (c + 1) + g < first - 1]
+            for g in ready[:2]:
                 weighted_sum_pass(c + 1, g)
             for a in range(V_TILES):
                 round_y(c, a)
-            decayed_momentum(c + 1, 0)
-            decayed_momentum(c + 1, 1)
+            decayed_momentum(c + 1)
             store_y(c, 0, V_TILES)
             if c + 3 < CHUNKS:
                 load_mom(c + 3)
@@ -334,35 +347,48 @@ def tile_relu_alignment_reweighted_gradients_k5_kernel(
             transpose_y(c, 2, 4)
             if c + 2 < CHUNKS:
                 spread_decay(c + 2)
-            done = ready
-            for i in range(first, first + STEP_TILES):
-                if i + 1 < TILES:
-                    if i > first:
-                        interleave_g_scalar(i + 1)
-                    interleave_g_vector(i + 1)
-                if i == first + 1:
-                    group_y(nc.scalar.copy, c, 0, 2)
-                    group_y(nc.scalar.copy, c, 2, 4)
-                if i == first + 2 and i + 1 < TILES:
-                    quantize_y(c, 0, V_TILES)
-                quantize_g(i)
-                while done < N_PASSES and N_PASSES * (c + 1) + done <= i:
-                    weighted_sum_pass(c + 1, done)
-                    done += 1
-        last = CHUNKS - 1
+            for g in ready[2:]:
+                weighted_sum_pass(c + 1, g)
+            quantize_g(first - 1, 0, HALF)
+            if c > 0:
+                quantize_y(c - 1, 0, V_TILES)
+            if full:
+                interleave_g("scalar", first + 1, 0, W)
+                quantize_g(first + 2, HALF, W)
+                quantize_g(first + 1, 0, W)
+                quantize_g(first, 0, W)
+            else:
+                interleave_g("scalar", first, 0, HALF)
+                quantize_g(first, HALF, W)
+                quantize_g(first, 0, HALF)
+            for g in range(len(ready), N_PASSES):
+                weighted_sum_pass(c + 1, g)
+        group_y(nc.scalar.copy, last - 1, 0, 2)
+        group_y(nc.scalar.copy, last - 1, 2, 4)
         quantize_y(last - 1, 0, V_TILES)
         store_y_scales(nc.sync, 0, last)
-        for a in range(V_TILES):
+        final = V_TILES - 1
+        for a in range(final):
             combine(last, a)
             round_y(last, a)
-            if a % 2 == 1:
-                store_y(last, a - 1, a + 1)
+        for u in range(2):
+            nc.vector.scalar_tensor_tensor(
+                out=pair_major(y_bf[last][:, final, :])[:, u],
+                in0=pair_order(u_ps[last, final][:])[:, u],
+                scalar=inv_mass[:, final : final + 1],
+                in1=pair_order(y[last][:, final, :])[:, u],
+                op0=ALU.mult,
+                op1=ALU.add,
+            )
+        store_y(last, 0, final)
+        combine(last, final)
+        store_y(last, final, V_TILES)
         transpose_y(last, 0, 2)
         transpose_y(last, 2, 3)
-        transpose_y(last, 3, 4)
-        group_y(nc.vector.tensor_copy, last, 0, 2)
-        group_y(nc.vector.tensor_copy, last, 2, 3)
+        turn(("y", last), y_bf[last], final, V_TILES, "acc", 5)
+        group_y(nc.scalar.copy, last, 0, 2)
+        group_y(nc.scalar.copy, last, 2, 3)
+        group_y(nc.vector.tensor_copy, last, final, V_TILES)
         quantize_y(last, 0, 2)
-        group_y(nc.vector.tensor_copy, last, 3, 4)
-        quantize_y(last, 2, 4)
+        quantize_y(last, 2, V_TILES)
         store_y_scales(nc.scalar, last, CHUNKS)

@@ -42,7 +42,7 @@ def tile_relu_alignment_reweighted_gradients_k5_kernel(
         inv_mass = keep.tile([P, V_TILES], F32, name="inv_mass")
         b_words = keep.tile([P, K1_PASSES, 2 * V], U8, name="b_words", align_bytes=64)
         b_scales = keep.tile([P, K1_PASSES, V], U8, name="b_scales", align_bytes=64)
-        a_scales = keep.tile([P, K1_PASSES, N], U8, name="a_scales", align_bytes=64)
+        a_scales = [keep.tile([P, K1_PASSES, n], U8, name="a_scales%d" % n, align_bytes=64) for n in (W, N - W)]
         a_words = [keep.tile([P, K1_PASSES, 2 * W], U8, name="a_words%d" % g, align_bytes=64) for g in range(N_PASSES)]
         offset_all = keep.tile([P, N], BF16, name="offset_all")
         r_codes = keep.tile([P, N_PASSES, V], I32, name="r_codes", align_bytes=64)
@@ -65,7 +65,7 @@ def tile_relu_alignment_reweighted_gradients_k5_kernel(
             nc.sync.dma_start(out=a_words[g][:].bitcast(I32), in_=src.bitcast(I32))
 
         def load_grad(c, g, chunks):
-            raw = work.tile([P, PACK, W * chunks], BF16, name="g_raw", tag="g_raw", bufs=8)
+            raw = work.tile([P, PACK, W * chunks], BF16, name="g_raw", tag="g_raw%d" % chunks, bufs=(4, 6)[chunks - 1])
             src = grad[W * g : W * (g + 1), W * c : W * (c + chunks)].rearrange("(p t) d -> p t d", t=PACK)
             nc.sync.dma_start(out=raw[:], in_=src)
             for i in range(chunks):
@@ -119,7 +119,7 @@ def tile_relu_alignment_reweighted_gradients_k5_kernel(
                     lhsT=b_words[:, k, 2 * P * a : 2 * P * (a + 1)].bitcast(FP4X4),
                     lhsT_scale=b_scales[:, k, P * a : P * (a + 1)],
                     rhs=a_words[g][:, k, :].bitcast(FP4X4),
-                    rhs_scale=a_scales[:, k, W * g : W * (g + 1)],
+                    rhs_scale=a_scales[0][:, k, :] if g == 0 else a_scales[1][:, k, W * (g - 1) : W * g],
                     start=(k == 0),
                     stop=(k == K1_PASSES - 1),
                 )
@@ -173,8 +173,8 @@ def tile_relu_alignment_reweighted_gradients_k5_kernel(
                 g_scales[order[i]] = work.tile([P, W], U8, name="g_scales", tag="g_scales", bufs=9, align_bytes=64)
             quantize(g_codes[order[i]][:, lo:hi], g_scales[order[i]][:, lo:hi], g_grouped[i, lo][:])
 
-        def weighted_sum_pass(c, g):
-            for a in range(V_TILES):
+        def weighted_sum_pass(c, g, tiles=range(V_TILES)):
+            for a in tiles:
                 if g == 0:
                     u_ps[c, a] = psum.tile([P, W], F32, name="u_ps", tag="acc", bufs=5)
                 nc.tensor.matmul_mx(
@@ -194,12 +194,26 @@ def tile_relu_alignment_reweighted_gradients_k5_kernel(
                 column = cols[:, block, row : row + 1].to_broadcast([P, P])
                 nc.tensor.transpose(decay_ps[c][:, P * s : P * (s + 1)], column, ident_bf[:])
 
-        def decayed_momentum(c):
-            y[c] = work.tile([P, V_TILES, W], F32, name="y", tag="y", bufs=3)
+        def y_tile(c):
+            if c not in y:
+                y[c] = work.tile([P, V_TILES, W], F32, name="y", tag="y", bufs=3)
+            return y[c]
+
+        def decayed_momentum(c, lo=0):
             nc.vector.tensor_tensor(
-                out=y[c][:],
-                in0=decay_ps[c][:].unsqueeze(1).to_broadcast([P, V_TILES, W]),
-                in1=mom_sb[c][:],
+                out=y_tile(c)[:, lo:, :],
+                in0=decay_ps[c][:].unsqueeze(1).to_broadcast([P, V_TILES - lo, W]),
+                in1=mom_sb[c][:, lo:, :],
+                op=ALU.mult,
+            )
+
+        def decayed_momentum_gpsimd(c, lo, hi):
+            decay_sb = keep.tile([P, W], BF16, name="decay_sb")
+            nc.scalar.copy(out=decay_sb[:], in_=decay_ps[c][:])
+            nc.gpsimd.tensor_tensor(
+                out=y_tile(c)[:, lo:hi, :],
+                in0=decay_sb[:].unsqueeze(1).to_broadcast([P, hi - lo, W]),
+                in1=mom_sb[c][:, lo:hi, :],
                 op=ALU.mult,
             )
 
@@ -252,18 +266,25 @@ def tile_relu_alignment_reweighted_gradients_k5_kernel(
 
         nc.scalar.dma_start(out=offset_cols[:], in_=offset.rearrange("(p s) -> p s", p=P))
         make_identity(nc, ident_f32[:])
-        nc.vector.memset(b_scales[:].bitcast(I32), 0)
-        nc.vector.memset(a_scales[:].bitcast(I32), 0)
-        nc.vector.memset(rows[:].bitcast(I32), 0)
         nc.scalar.copy(out=ident_bf[:], in_=ident_f32[:])
+        nc.vector.memset(a_scales[0][:].bitcast(I32), 0)
+        nc.vector.memset(b_scales[:].bitcast(I32), 0)
+        nc.vector.memset(a_scales[1][:].bitcast(I32), 0)
+        nc.vector.memset(rows[:].bitcast(I32), 0)
+        load_scale_rows(nc.gpsimd, a_scales[1], train_scales[:, :, W:N], range(4))
         nc.sync.dma_start(out=b_words[:].bitcast(I32), in_=val_words.rearrange("k p b -> p k b").bitcast(I32))
+        load_scale_rows(nc.sync, a_scales[0], train_scales[:, :, 0:W], range(4))
         load_a_words(0)
         load_scale_rows(nc.sync, b_scales, val_scales, range(4))
-        load_scale_rows(nc.sync, a_scales, train_scales, range(4))
         for g in range(N_PASSES):
-            load_grad(0, g, 2)
-            if g + 1 < N_PASSES:
+            if g < 2:
+                load_grad(0, g, 1)
                 load_a_words(g + 1)
+                load_grad(1, g, 1)
+            else:
+                load_grad(0, g, 2)
+                if g + 1 < N_PASSES:
+                    load_a_words(g + 1)
             if g == 1:
                 nc.sync.dma_start(out=rows[0:4, 0:CHUNKS, :], in_=decay.rearrange("(r b d) -> r b d", r=4, d=P))
                 nc.sync.dma_start(out=rows[0:4, CHUNKS, :], in_=mass.rearrange("(a p) -> a p", p=P))
@@ -304,8 +325,10 @@ def tile_relu_alignment_reweighted_gradients_k5_kernel(
         group_r(last_pass)
         weighted_sum_pass(0, 1)
         weighted_sum_pass(0, 2)
-        interleave_g("gpsimd", 9, HALF, W, "lead")
-        interleave_g("scalar", 8, 0, W)
+        for g in range(last_pass):
+            weighted_sum_pass(1, g, range(1))
+        interleave_g("gpsimd", 8, HALF, W, "lead")
+        interleave_g("scalar", 8, 0, HALF)
         nc.vector.reciprocal(out=inv_mass[:], in_=cols[:, CHUNKS, :])
         decayed_momentum(0)
         relu_r(last_pass)
@@ -313,8 +336,9 @@ def tile_relu_alignment_reweighted_gradients_k5_kernel(
         quantize_r(last_pass)
         weighted_sum_pass(0, last_pass)
         spread_decay(1)
-        quantize_g(8, 0, W)
-        quantize_g(9, HALF, W)
+        interleave_g("scalar", 9, 0, W)
+        quantize_g(8, 0, HALF)
+        quantize_g(8, HALF, W)
         load_mom(2)
         for g in range(N_PASSES):
             load_grad(CHUNKS - 1, g, 1)
@@ -324,47 +348,42 @@ def tile_relu_alignment_reweighted_gradients_k5_kernel(
             first = 10 + 3 * c
             full = c + 1 < last
             if full:
-                interleave_g("gpsimd", first, 0, W, "lead")
-                interleave_g("gpsimd", first + 2, HALF, W, "second")
+                interleave_g("gpsimd", first + 1, 0, W, "lead")
+                interleave_g("gpsimd", first, HALF, W, "second")
             else:
                 interleave_g("gpsimd", first, HALF, W, "lead")
-            interleave_g("scalar", first - 1, 0, HALF)
-            if c > 0:
-                group_y(nc.scalar.copy, c - 1, 0, 2)
-                group_y(nc.scalar.copy, c - 1, 2, 4)
+                decayed_momentum_gpsimd(last, 0, 1)
+            interleave_g("scalar", first, 0, HALF)
             for a in range(V_TILES):
                 combine(c, a)
             ready = [g for g in range(N_PASSES) if N_PASSES * (c + 1) + g < first - 1]
             for g in ready[:2]:
-                weighted_sum_pass(c + 1, g)
+                weighted_sum_pass(c + 1, g, range(1 if c == 0 and g < last_pass else 0, V_TILES))
             for a in range(V_TILES):
                 round_y(c, a)
-            decayed_momentum(c + 1)
+            decayed_momentum(c + 1, 0 if full else 1)
             store_y(c, 0, V_TILES)
             if c + 3 < CHUNKS:
                 load_mom(c + 3)
             transpose_y(c, 0, 2)
             transpose_y(c, 2, 4)
+            for g in ready[2:]:
+                weighted_sum_pass(c + 1, g, range(1 if c == 0 and g < last_pass else 0, V_TILES))
             if c + 2 < CHUNKS:
                 spread_decay(c + 2)
-            for g in ready[2:]:
-                weighted_sum_pass(c + 1, g)
-            quantize_g(first - 1, 0, HALF)
+            quantize_g(first - 1, 0, W)
+            if full:
+                interleave_g("scalar", first + 2, 0, W)
+            group_y(nc.scalar.copy, c, 0, 2)
+            group_y(nc.scalar.copy, c, 2, 4)
+            quantize_g(first, 0, HALF)
+            quantize_g(first, HALF, W)
             if c > 0:
                 quantize_y(c - 1, 0, V_TILES)
             if full:
-                interleave_g("scalar", first + 1, 0, W)
-                quantize_g(first + 2, HALF, W)
                 quantize_g(first + 1, 0, W)
-                quantize_g(first, 0, W)
-            else:
-                interleave_g("scalar", first, 0, HALF)
-                quantize_g(first, HALF, W)
-                quantize_g(first, 0, HALF)
             for g in range(len(ready), N_PASSES):
-                weighted_sum_pass(c + 1, g)
-        group_y(nc.scalar.copy, last - 1, 0, 2)
-        group_y(nc.scalar.copy, last - 1, 2, 4)
+                weighted_sum_pass(c + 1, g, range(1 if c == 0 and g < last_pass else 0, V_TILES))
         quantize_y(last - 1, 0, V_TILES)
         store_y_scales(nc.sync, 0, last)
         final = V_TILES - 1

@@ -42,7 +42,7 @@ def tile_relu_alignment_reweighted_gradients_k5_kernel(
         inv_mass = keep.tile([P, V_TILES], F32, name="inv_mass")
         b_words = keep.tile([P, K1_PASSES, 2 * V], U8, name="b_words", align_bytes=64)
         b_scales = keep.tile([P, K1_PASSES, V], U8, name="b_scales", align_bytes=64)
-        a_scales = [keep.tile([P, K1_PASSES, n], U8, name="a_scales%d" % n, align_bytes=64) for n in (W, N - W)]
+        a_scales = [keep.tile([P, K1_PASSES, N // 2], U8, name="a_scales%d" % h, align_bytes=64) for h in range(2)]
         a_words = [keep.tile([P, K1_PASSES, 2 * W], U8, name="a_words%d" % g, align_bytes=64) for g in range(N_PASSES)]
         offset_all = keep.tile([P, N], BF16, name="offset_all")
         r_codes = keep.tile([P, N_PASSES, V], I32, name="r_codes", align_bytes=64)
@@ -119,7 +119,7 @@ def tile_relu_alignment_reweighted_gradients_k5_kernel(
                     lhsT=b_words[:, k, 2 * P * a : 2 * P * (a + 1)].bitcast(FP4X4),
                     lhsT_scale=b_scales[:, k, P * a : P * (a + 1)],
                     rhs=a_words[g][:, k, :].bitcast(FP4X4),
-                    rhs_scale=a_scales[0][:, k, :] if g == 0 else a_scales[1][:, k, W * (g - 1) : W * g],
+                    rhs_scale=a_scales[g // 2][:, k, W * (g % 2) : W * (g % 2 + 1)],
                     start=(k == 0),
                     stop=(k == K1_PASSES - 1),
                 )
@@ -267,15 +267,15 @@ def tile_relu_alignment_reweighted_gradients_k5_kernel(
         nc.scalar.dma_start(out=offset_cols[:], in_=offset.rearrange("(p s) -> p s", p=P))
         make_identity(nc, ident_f32[:])
         nc.scalar.copy(out=ident_bf[:], in_=ident_f32[:])
-        nc.vector.memset(a_scales[0][:].bitcast(I32), 0)
         nc.vector.memset(b_scales[:].bitcast(I32), 0)
+        nc.vector.memset(a_scales[0][:].bitcast(I32), 0)
         nc.vector.memset(a_scales[1][:].bitcast(I32), 0)
         nc.vector.memset(rows[:].bitcast(I32), 0)
-        load_scale_rows(nc.gpsimd, a_scales[1], train_scales[:, :, W:N], range(4))
+        load_scale_rows(nc.gpsimd, a_scales[1], train_scales[:, :, N // 2 : N], range(4))
         nc.sync.dma_start(out=b_words[:].bitcast(I32), in_=val_words.rearrange("k p b -> p k b").bitcast(I32))
-        load_scale_rows(nc.sync, a_scales[0], train_scales[:, :, 0:W], range(4))
-        load_a_words(0)
         load_scale_rows(nc.sync, b_scales, val_scales, range(4))
+        load_a_words(0)
+        load_scale_rows(nc.sync, a_scales[0], train_scales[:, :, 0 : N // 2], range(4))
         for g in range(N_PASSES):
             if g < 2:
                 load_grad(0, g, 1)

from contextlib import ExitStack

import concourse.mybir as mybir
from concourse.masks import make_identity

V, N, K1, D = 512, 2048, 1536, 2560
FLOPS = 2 * K1 * N * V + 2 * N * V * D

F32 = mybir.dt.float32
BF16 = mybir.dt.bfloat16
I32 = mybir.dt.int32
U8 = mybir.dt.uint8
FP8X4 = mybir.dt.float8_e4m3fn_x4
FP4X4 = mybir.dt.float4_e2m1fn_x4
ALU = mybir.AluOpType
ACT = mybir.ActivationFunctionType

P = 128
PACK = 4
W = 512
K1_PASSES = K1 // W
N_PASSES = N // W
CHUNKS = D // W
V_TILES = V // P
HALF = W // 2

def tile_relu_alignment_reweighted_gradients_k5_kernel(
    tc, train_words, train_scales, val_words, val_scales, offset, grad, mass, decay, mom, out_0, out_1, out_2
):
    nc = tc.nc
    with ExitStack() as ctx:
        keep = ctx.enter_context(tc.tile_pool(name="keep", bufs=1))
        work = ctx.enter_context(tc.tile_pool(name="work", bufs=2))
        psum = ctx.enter_context(tc.psum_pool(name="psum", bufs=1))
        ctx.enter_context(tc.manual_schedule())

        ident_bf = keep.tile([P, P], BF16, name="ident_bf")
        ident_f32 = keep.tile([P, P], F32, name="ident_f32")
        offset_cols = keep.tile([P, N // P], BF16, name="offset_cols")
        rows = keep.tile([P, CHUNKS + 1, P], BF16, name="rows")
        cols = keep.tile([P, CHUNKS + 1, 4], BF16, name="cols")
        inv_mass = keep.tile([P, V_TILES], F32, name="inv_mass")
        b_words = keep.tile([P, K1_PASSES, 2 * V], U8, name="b_words", align_bytes=64)
        b_scales = keep.tile([P, K1_PASSES, V], U8, name="b_scales", align_bytes=64)
        a_scales = [keep.tile([P, K1_PASSES, N // 2], U8, name="a_scales%d" % h, align_bytes=64) for h in range(2)]
        a_words = [keep.tile([P, K1_PASSES, 2 * W], U8, name="a_words%d" % g, align_bytes=64) for g in range(N_PASSES)]
        offset_all = keep.tile([P, N], BF16, name="offset_all")
        r_codes = keep.tile([P, N_PASSES, V], I32, name="r_codes", align_bytes=64)
        r_scales = keep.tile([P, N_PASSES, V], U8, name="r_scales", align_bytes=64)
        y_scales = keep.tile([P, CHUNKS, V], U8, name="y_scales", align_bytes=64)

        order = [(c, g) for g in range(N_PASSES) for c in range(2)]
        order += [(c, g) for c in range(2, CHUNKS) for g in range(N_PASSES)]
        z_bf, r_grouped, turned = {}, {}, {}
        g_raw, g_grouped, g_codes, g_scales = {}, {}, {}, {}
        mom_sb, decay_ps, y, y_bf, y_grouped, y_codes, u_ps = {}, {}, {}, {}, {}, {}, {}

        def load_scale_rows(queue, plane, scales, rows_of_four):
            by_row = scales.rearrange("k (q r) n -> r q k n", r=4)
            for r in rows_of_four:
                queue.dma_start(out=plane[r:P:32, :, :].bitcast(I32), in_=by_row[r].bitcast(I32))

        def load_a_words(g):
            src = train_words[:, :, 2 * W * g : 2 * W * (g + 1)].rearrange("k p b -> p k b")
            nc.sync.dma_start(out=a_words[g][:].bitcast(I32), in_=src.bitcast(I32))

        def load_grad(c, g, chunks):
            raw = work.tile([P, PACK, W * chunks], BF16, name="g_raw", tag="g_raw%d" % chunks, bufs=(4, 6)[chunks - 1])
            src = grad[W * g : W * (g + 1), W * c : W * (c + chunks)].rearrange("(p t) d -> p t d", t=PACK)
            nc.sync.dma_start(out=raw[:], in_=src)
            for i in range(chunks):
                g_raw[c + i, g] = raw[:, :, W * i : W * (i + 1)]

        def load_mom(c):
            mom_sb[c] = work.tile([P, V_TILES, W], BF16, name="mom_sb", tag="mom_sb", bufs=3)
            nc.sync.dma_start(out=mom_sb[c][:], in_=mom[:, W * c : W * (c + 1)].rearrange("(a p) d -> p a d", p=P))

        def grouped_tile(width):
            return work.tile([P, width, PACK], BF16, name="grouped", tag="grouped", bufs=5, align_bytes=64)

        def quantize(codes, scales, grouped):
            nc.vector.quantize_mx(out=codes.bitcast(FP8X4), scales=scales, in_=grouped.rearrange("p w t -> p (w t)"))

        def pair_order(ap):
            return ap.rearrange("p (m u e) -> p u m e", u=2, e=2)

        def pair_major(ap):
            return ap.rearrange("p (u m e) -> p u m e", u=2, e=2)

        def rounded_tile():
            return work.tile([P, V_TILES, W], BF16, name="rounded", tag="rounded", bufs=3)

        def turn(key, rounded, lo, hi, tag="turned", bufs=2):
            turned[key, lo] = psum.tile([P, hi - lo, 2, P], F32, name="turned", tag=tag, bufs=bufs)
            for a in range(lo, hi):
                pairs = rounded[:, a, :].bitcast(F32)
                for u in range(2):
                    nc.tensor.transpose(turned[key, lo][:, a - lo, u, :], pairs[:, P * u : P * (u + 1)], ident_f32[:])

        def group(copy, key, grouped, lo, hi):
            dst = grouped[:, P * lo : P * hi, :].bitcast(F32)
            copy(out=dst.rearrange("p (a v) u -> p a v u", v=P), in_=turned[key, lo][:].rearrange("p a u v -> p a v u"))

        def spread_offset(half):
            spread = psum.tile([P, 4, P], F32, name="spread", tag="turned", bufs=2)
            for s in range(4):
                column = offset_cols[:].bitcast(F32)[:, 4 * half + s : 4 * half + s + 1].to_broadcast([P, P])
                nc.tensor.transpose(spread[:, s, :], column, ident_f32[:])
            dst = offset_all[:].bitcast(F32).rearrange("p (k s) -> p k s", s=8)[:, :, 4 * half : 4 * half + 4]
            nc.scalar.copy(out=dst, in_=spread[:].rearrange("p s k -> p k s"))

        def alignment(g, a):
            if a == 0:
                z_bf[g] = rounded_tile()
            s_ps = psum.tile([P, W], F32, name="s_ps", tag="acc", bufs=5)
            for k in range(K1_PASSES):
                nc.tensor.matmul_mx(
                    out=s_ps[:],
                    lhsT=b_words[:, k, 2 * P * a : 2 * P * (a + 1)].bitcast(FP4X4),
                    lhsT_scale=b_scales[:, k, P * a : P * (a + 1)],
                    rhs=a_words[g][:, k, :].bitcast(FP4X4),
                    rhs_scale=a_scales[g // 2][:, k, W * (g % 2) : W * (g % 2 + 1)],
                    start=(k == 0),
                    stop=(k == K1_PASSES - 1),
                )
            nc.vector.tensor_tensor(
                out=pair_major(z_bf[g][:, a, :]),
                in0=pair_order(s_ps[:]),
                in1=pair_order(offset_all[:, W * g : W * (g + 1)]),
                op=ALU.add,
            )

        def turn_r(g):
            for lo in (0, 2):
                turn(("r", g), z_bf[g], lo, lo + 2)

        def group_r(g):
            r_grouped[g] = grouped_tile(V)
            for lo in (0, 2):
                group(nc.scalar.copy, ("r", g), r_grouped[g], lo, lo + 2)

        def relu_r(g):
            flat = r_grouped[g][:].rearrange("p w t -> p (w t)")
            nc.vector.tensor_scalar(out=flat, in0=flat, scalar1=0.0, scalar2=None, op0=ALU.max)

        def quantize_r(g):
            quantize(r_codes[:, g, :], r_scales[:, g, :], r_grouped[g][:])

        def interleave_g(engine, i, lo, hi, tag="grouped"):
            raw = g_raw[order[i]]
            if engine == "gpsimd":
                grouped = work.tile([P, hi - lo, PACK], BF16, name=tag, tag=tag, bufs=1, align_bytes=64)
                nc.gpsimd.tensor_scalar(
                    out=grouped[:],
                    in0=raw[:, :, lo:hi].rearrange("p t w -> p w t"),
                    scalar1=1.0,
                    scalar2=0.0,
                    op0=ALU.mult,
                    op1=ALU.add,
                )
            else:
                grouped = grouped_tile(hi - lo)
                copy = nc.scalar.copy if engine == "scalar" else nc.vector.tensor_copy
                copy(
                    out=grouped[:].rearrange("p (c i) t -> p c t i", i=4),
                    in_=raw[:, :, lo:hi].rearrange("p t (c i) -> p c t i", i=4),
                )
            g_grouped[i, lo] = grouped

        def quantize_g(i, lo, hi):
            if order[i] not in g_codes:
                g_codes[order[i]] = work.tile([P, W], I32, name="g_codes", tag="g_codes", bufs=9, align_bytes=64)
                g_scales[order[i]] = work.tile([P, W], U8, name="g_scales", tag="g_scales", bufs=9, align_bytes=64)
            quantize(g_codes[order[i]][:, lo:hi], g_scales[order[i]][:, lo:hi], g_grouped[i, lo][:])

        def weighted_sum_pass(c, g, tiles=range(V_TILES)):
            for a in tiles:
                if g == 0:
                    u_ps[c, a] = psum.tile([P, W], F32, name="u_ps", tag="acc", bufs=5)
                nc.tensor.matmul_mx(
                    out=u_ps[c, a][:],
                    lhsT=r_codes[:, g, P * a : P * (a + 1)].bitcast(FP8X4),
                    lhsT_scale=r_scales[:, g, P * a : P * (a + 1)],
                    rhs=g_codes[c, g][:].bitcast(FP8X4),
                    rhs_scale=g_scales[c, g][:],
                    start=(g == 0),
                    stop=(g == N_PASSES - 1),
                )

        def spread_decay(c):
            decay_ps[c] = psum.tile([P, W], BF16, name="decay_ps", tag="decay_ps")
            for s in range(PACK):
                row, block = divmod(PACK * c + s, CHUNKS)
                column = cols[:, block, row : row + 1].to_broadcast([P, P])
                nc.tensor.transpose(decay_ps[c][:, P * s : P * (s + 1)], column, ident_bf[:])

        def y_tile(c):
            if c not in y:
                y[c] = work.tile([P, V_TILES, W], F32, name="y", tag="y", bufs=3)
            return y[c]

        def decayed_momentum(c, lo=0):
            nc.vector.tensor_tensor(
                out=y_tile(c)[:, lo:, :],
                in0=decay_ps[c][:].unsqueeze(1).to_broadcast([P, V_TILES - lo, W]),
                in1=mom_sb[c][:, lo:, :],
                op=ALU.mult,
            )

        def decayed_momentum_gpsimd(c, lo, hi):
            decay_sb = keep.tile([P, W], BF16, name="decay_sb")
            nc.scalar.copy(out=decay_sb[:], in_=decay_ps[c][:])
            nc.gpsimd.tensor_tensor(
                out=y_tile(c)[:, lo:hi, :],
                in0=decay_sb[:].unsqueeze(1).to_broadcast([P, hi - lo, W]),
                in1=mom_sb[c][:, lo:hi, :],
                op=ALU.mult,
            )

        def combine(c, a):
            nc.vector.scalar_tensor_tensor(
                out=y[c][:, a, :],
                in0=u_ps[c, a][:],
                scalar=inv_mass[:, a : a + 1],
                in1=y[c][:, a, :],
                op0=ALU.mult,
                op1=ALU.add,
            )

        def store_y(c, lo, hi):
            dst = out_0[:, W * c : W * (c + 1)].rearrange("(a p) d -> p a d", p=P)
            nc.sync.dma_start(out=dst[:, lo:hi, :], in_=y[c][:, lo:hi, :])

        def round_y(c, a):
            if a == 0:
                y_bf[c] = rounded_tile()
            dst, src = pair_major(y_bf[c][:, a, :]), pair_order(y[c][:, a, :])
            nc.scalar.copy(out=dst, in_=src)

        def transpose_y(c, lo, hi):
            turn(("y", c), y_bf[c], lo, hi)

        def group_y(copy, c, lo, hi):
            if lo == 0:
                y_grouped[c] = work.tile([P, V, PACK], BF16, name="y_grouped", tag="y_grouped", align_bytes=64)
            group(copy, ("y", c), y_grouped[c], lo, hi)

        def quantize_y(c, lo, hi):
            if lo == 0:
                y_codes[c] = work.tile([P, V], I32, name="y_codes", tag="y_codes", align_bytes=64)
            span = slice(P * lo, P * hi)
            quantize(y_codes[c][:, span], y_scales[:, c, span], y_grouped[c][:, span, :])
            dst = out_1[c].rearrange("p m t -> p (m t)").bitcast(I32)
            nc.sync.dma_start(out=dst[:, span], in_=y_codes[c][:, span])

        def store_y_scales(queue, lo, hi):
            for q in range(4):
                dst = out_2[lo:hi, 4 * q : 4 * q + 4, :].rearrange("c r m -> r c m")
                queue.dma_start(out=dst.bitcast(I32), in_=y_scales[32 * q : 32 * q + 4, lo:hi, :].bitcast(I32))

        def turn_rows():
            rows_t = psum.tile([P, CHUNKS + 1, P], BF16, name="rows_t", tag="decay_ps")
            for s in range(CHUNKS + 1):
                nc.tensor.transpose(rows_t[:, s, :], rows[:, s, :], ident_bf[:])
            nc.scalar.copy(out=cols[:], in_=rows_t[:, :, 0:4])

        nc.scalar.dma_start(out=offset_cols[:], in_=offset.rearrange("(p s) -> p s", p=P))
        make_identity(nc, ident_f32[:])
        nc.scalar.copy(out=ident_bf[:], in_=ident_f32[:])
        nc.vector.memset(b_scales[:].bitcast(I32), 0)
        nc.vector.memset(a_scales[0][:].bitcast(I32), 0)
        nc.vector.memset(a_scales[1][:].bitcast(I32), 0)
        nc.vector.memset(rows[:].bitcast(I32), 0)
        load_scale_rows(nc.gpsimd, a_scales[1], train_scales[:, :, N // 2 : N], range(4))
        nc.sync.dma_start(out=b_words[:].bitcast(I32), in_=val_words.rearrange("k p b -> p k b").bitcast(I32))
        load_scale_rows(nc.sync, b_scales, val_scales, range(4))
        load_a_words(0)
        load_scale_rows(nc.sync, a_scales[0], train_scales[:, :, 0 : N // 2], range(4))
        for g in range(N_PASSES):
            if g < 2:
                load_grad(0, g, 1)
                load_a_words(g + 1)
                load_grad(1, g, 1)
            else:
                load_grad(0, g, 2)
                if g + 1 < N_PASSES:
                    load_a_words(g + 1)
            if g == 1:
                nc.sync.dma_start(out=rows[0:4, 0:CHUNKS, :], in_=decay.rearrange("(r b d) -> r b d", r=4, d=P))
                nc.sync.dma_start(out=rows[0:4, CHUNKS, :], in_=mass.rearrange("(a p) -> a p", p=P))
            if g == 2:
                load_mom(0)
        load_grad(2, 0, 2)
        load_mom(1)
        for g in range(1, N_PASSES):
            load_grad(2, g, 2)

        spread_offset(0)
        spread_offset(1)

        for g in range(N_PASSES):
            interleave_g("scalar", 2 * g, 0, W)
            interleave_g("gpsimd", 2 * g + 1, HALF, W, "lead")
            alignment(g, 0)
            alignment(g, 1)
            if g > 0:
                turn_r(g - 1)
                group_r(g - 1)
            alignment(g, 2)
            alignment(g, 3)
            if g == 2:
                turn_rows()
            if g > 0:
                quantize_g(2 * g - 1, 0, HALF)
                relu_r(g - 1)
            interleave_g("scalar", 2 * g + 1, 0, HALF)
            quantize_g(2 * g, 0, W)
            if g > 0:
                quantize_r(g - 1)
            quantize_g(2 * g + 1, HALF, W)
        last_pass = N_PASSES - 1
        spread_decay(0)
        weighted_sum_pass(0, 0)
        turn_r(last_pass)
        group_r(last_pass)
        weighted_sum_pass(0, 1)
        weighted_sum_pass(0, 2)
        for g in range(last_pass):
            weighted_sum_pass(1, g, range(1))
        interleave_g("gpsimd", 8, HALF, W, "lead")
        interleave_g("scalar", 8, 0, HALF)
        nc.vector.reciprocal(out=inv_mass[:], in_=cols[:, CHUNKS, :])
        decayed_momentum(0)
        relu_r(last_pass)
        quantize_g(7, 0, HALF)
        quantize_r(last_pass)
        weighted_sum_pass(0, last_pass)
        spread_decay(1)
        interleave_g("scalar", 9, 0, W)
        quantize_g(8, 0, HALF)
        quantize_g(8, HALF, W)
        load_mom(2)
        for g in range(N_PASSES):
            load_grad(CHUNKS - 1, g, 1)

        last = CHUNKS - 1
        for c in range(last):
            first = 10 + 3 * c
            full = c + 1 < last
            if full:
                interleave_g("gpsimd", first + 1, 0, W, "lead")
                interleave_g("gpsimd", first, HALF, W, "second")
            else:
                interleave_g("gpsimd", first, HALF, W, "lead")
                decayed_momentum_gpsimd(last, 0, 1)
            interleave_g("scalar", first, 0, HALF)
            for a in range(V_TILES):
                combine(c, a)
            ready = [g for g in range(N_PASSES) if N_PASSES * (c + 1) + g < first - 1]
            for g in ready[:2]:
                weighted_sum_pass(c + 1, g, range(1 if c == 0 and g < last_pass else 0, V_TILES))
            for a in range(V_TILES):
                round_y(c, a)
            decayed_momentum(c + 1, 0 if full else 1)
            store_y(c, 0, V_TILES)
            if c + 3 < CHUNKS:
                load_mom(c + 3)
            transpose_y(c, 0, 2)
            transpose_y(c, 2, 4)
            for g in ready[2:]:
                weighted_sum_pass(c + 1, g, range(1 if c == 0 and g < last_pass else 0, V_TILES))
            if c + 2 < CHUNKS:
                spread_decay(c + 2)
            quantize_g(first - 1, 0, W)
            if full:
                interleave_g("scalar", first + 2, 0, W)
            group_y(nc.scalar.copy, c, 0, 2)
            group_y(nc.scalar.copy, c, 2, 4)
            quantize_g(first, 0, HALF)
            quantize_g(first, HALF, W)
            if c > 0:
                quantize_y(c - 1, 0, V_TILES)
            if full:
                quantize_g(first + 1, 0, W)
            for g in range(len(ready), N_PASSES):
                weighted_sum_pass(c + 1, g, range(1 if c == 0 and g < last_pass else 0, V_TILES))
        quantize_y(last - 1, 0, V_TILES)
        store_y_scales(nc.sync, 0, last)
        final = V_TILES - 1
        for a in range(final):
            combine(last, a)
            round_y(last, a)
        for u in range(2):
            nc.vector.scalar_tensor_tensor(
                out=pair_major(y_bf[last][:, final, :])[:, u],
                in0=pair_order(u_ps[last, final][:])[:, u],
                scalar=inv_mass[:, final : final + 1],
                in1=pair_order(y[last][:, final, :])[:, u],
                op0=ALU.mult,
                op1=ALU.add,
            )
        store_y(last, 0, final)
        combine(last, final)
        store_y(last, final, V_TILES)
        transpose_y(last, 0, 2)
        transpose_y(last, 2, 3)
        turn(("y", last), y_bf[last], final, V_TILES, "acc", 5)
        group_y(nc.scalar.copy, last, 0, 2)
        group_y(nc.scalar.copy, last, 2, 3)
        group_y(nc.vector.tensor_copy, last, final, V_TILES)
        quantize_y(last, 0, 2)
        quantize_y(last, 2, V_TILES)
        store_y_scales(nc.scalar, last, CHUNKS)
